import numpy as np
import ml_dtypes


def mxq(x, axis, fmt="e4m3"):
    dtype, down = {"e4m3": (ml_dtypes.float8_e4m3fn, 7), "e5m2": (ml_dtypes.float8_e5m2, 14)}[fmt]
    v = np.moveaxis(np.asarray(x, np.float32).astype(ml_dtypes.bfloat16).astype(np.float64), axis, -1)
    blocks = v.reshape(v.shape[:-1] + (-1, 32))
    amax = np.abs(blocks).max(-1, keepdims=True)
    byte = np.maximum(np.where(amax > 0, np.frexp(amax)[1] - 1 + 127, 0) - down, 1)
    scale = np.exp2(byte - 127.0)
    codes = (blocks / scale).astype(np.float32).astype(dtype).astype(np.float64)
    return np.moveaxis((codes * scale).reshape(v.shape), -1, axis)


WIDE = False


def mx_kscale(k):
    if not WIDE:
        return np.ones(k)
    levels = np.array([10, -10, 5, -5, 0])
    if k % 512:
        return np.exp2(np.random.permutation(np.resize(levels, k // 32))).repeat(32)
    a = np.empty((k // 512, 16))
    for p in range(k // 512):
        a[p, :8] = np.random.permutation(np.resize(levels, 8))
        for g in range(8):
            far = levels[np.abs(levels - a[p, g]) >= 10]
            a[p, g + 8] = far[np.random.randint(len(far))]
    return np.exp2(a.ravel()).repeat(32)


def f64(x):
    return np.asarray(x).astype(np.float64)


def striped(idx):
    return np.tile(idx.reshape(-1, 16).T, (8, 1)).astype(np.uint16)


def unstriped(offs):
    return offs[:16].T.reshape(-1).astype(np.int64)


E2M1 = np.array([0.0, 0.5, 1.0, 1.5, 2.0, 3.0, 4.0, 6.0, -0.0, -0.5, -1.0, -1.5, -2.0, -3.0, -4.0, -6.0])


def pack_weight(w, fmt):
    k, n = w.shape
    w = f64(np.asarray(w, np.float32).astype(ml_dtypes.bfloat16)).reshape(k // 32, 32, n)
    amax = np.abs(w).max(1)
    if fmt == "e4m3":
        byte = np.frexp(amax)[1] - 1 + 127 - 7
    else:
        mant, ex = np.frexp(amax / 6.0)
        byte = np.where(mant > 0.5, ex, ex - 1) + 127
    byte = np.clip(np.where(amax > 0, byte, 1), 1, 254)
    scaled = (w * np.exp2(127.0 - byte)[:, None, :]).reshape(k, n).astype(np.float32)
    by_word = np.ascontiguousarray(scaled.reshape(k // 512, 128, 4, n).transpose(0, 1, 3, 2))
    if fmt == "e4m3":
        words = by_word.astype(ml_dtypes.float8_e4m3fn).view(np.uint8)
    else:
        c = by_word.astype(ml_dtypes.float4_e2m1fn).view(np.uint8) & 0xF
        words = (c[..., 0::2] | (c[..., 1::2] << 4)).reshape(k // 512, 128, 2 * n)
    return np.ascontiguousarray(words), np.ascontiguousarray(byte.astype(np.uint8).reshape(k // 512, 16, n))


def unpack_weight(words, scales, fmt):
    g, _, n = scales.shape
    words = np.ascontiguousarray(words).reshape(g, 128, n, -1)
    if fmt == "e4m3":
        vals = words.view(ml_dtypes.float8_e4m3fn).astype(np.float64)
    else:
        nib = np.empty((g, 128, n, 4), np.uint8)
        nib[..., 0::2] = words & 0xF
        nib[..., 1::2] = words >> 4
        vals = E2M1[nib]
    vals = vals * np.repeat(np.exp2(scales.astype(np.float64) - 127.0), 8, axis=1)[..., None]
    return vals.transpose(0, 1, 3, 2).reshape(g * 512, n)


K, T, E, C, N = 1024, 1280, 15, 256, 128
TOP = 3


def by_expert(wq, xq):
    return np.concatenate([wq[e].T @ xq[:, e * C:(e + 1) * C] for e in range(E)], axis=1)


def setup_inputs():
    n = np.random.standard_normal
    s = mx_kscale(K)[:, None]
    deal = np.repeat(np.arange(E), C).reshape(TOP, T)[:, np.random.permutation(T)]
    deal = np.take_along_axis(deal, np.argsort(np.random.rand(TOP, T), axis=0), axis=0)
    for _ in range(8):
        s_, t_ = np.random.permutation(T).reshape(2, -1); r = np.random.randint(TOP, size=T // 2); x, y = deal[r, s_].copy(), deal[r, t_].copy()
        ok = ~((deal[:, s_] == y).any(0) | (deal[:, t_] == x).any(0)); deal[r[ok], s_[ok]] = y[ok]; deal[r[ok], t_[ok]] = x[ok]
    order = np.lexsort((np.random.rand(TOP * T), deal.reshape(-1)))
    slot_token = order % T; pos = np.empty(TOP * T, np.int64); pos[order] = np.arange(TOP * T); pos = pos.reshape(TOP, T)
    g = np.random.uniform(0.5, 1.5, (TOP, T)); g = g / g.sum(0)
    w = [pack_weight(m, "e2m1") for m in n((E, K, N)) / np.sqrt(K) / s[None]]
    w_slot = np.empty(E * C)
    for r in range(TOP): w_slot[pos[r]] = g[r]
    return {
        "xT": (n((K, T)) * s).astype(np.float32),
        "w_words": np.stack([m[0] for m in w]),
        "w_scales": np.stack([m[1] for m in w]),
        "b": (0.3 * n((N, E))).astype(np.float32),
        "gate": np.tile(w_slot, (K, 1)).astype(np.float32),
        "offs": striped(slot_token),
        "pos1": striped(pos[0]),
        "pos2": striped(pos[1]),
        "pos3": striped(pos[2]),
    }


def reference(xT, w_words, w_scales, b, gate, offs, pos1, pos2, pos3):
    idx = unstriped(offs)
    w = np.stack([unpack_weight(w_words[e], w_scales[e], "e2m1") for e in range(E)])
    xq = mxq(f64(gate) * f64(xT)[:, idx], 0, "e4m3")
    y = by_expert(w, xq)
    y = y + np.repeat(f64(b), C, axis=1)
    return y[:, unstriped(pos1)] + y[:, unstriped(pos2)] + y[:, unstriped(pos3)]

@@ -1,0 +1,165 @@
+from contextlib import ExitStack
+
+import concourse.mybir as mybir
+
+K, T, E, C, N = 1024, 1280, 15, 256, 128
+S = E * C
+FLOPS = 2 * K * N * S
+BYTES = 4 * K * T + E * K * N // 2 + E * K * N // 32 + 4 * N * E + 4 * S + 2 * 128 * (S + 3 * T) // 16 + 4 * N * T
+
+F32 = mybir.dt.float32
+BF16 = mybir.dt.bfloat16
+I32 = mybir.dt.int32
+U32 = mybir.dt.uint32
+U16 = mybir.dt.uint16
+U8 = mybir.dt.uint8
+FP8X4 = mybir.dt.float8_e4m3fn_x4
+FP4X4 = mybir.dt.float4_e2m1fn_x4
+MULT = mybir.AluOpType.mult
+ADD = mybir.AluOpType.add
+IDENT = mybir.ActivationFunctionType.Identity
+
+P = 128
+PACK = 4
+PASSES = K // (P * PACK)
+STRIPE = 16
+UNITS = [(0, 0, 1024), (1, 0, 1024), (0, 1024, 1024), (1, 1024, 1024), (0, 2048, 1024), (1, 2048, 1024), (0, 3072, 768), (1, 3072, 384), (1, 3456, 256), (1, 3712, 128)]
+GATE_LOADS = [(0, 256), (256, 768), (1024, 1024), (2048, 1792)]
+HALF = T // 2
+OUT_PIECES = [(0, 512), (512, 512), (1024, 256)]
+W_GROUP = 5
+
+
+def tile_moe_pre_lin_bias_kernel(tc, xT, w_words, w_scales, b, gate, offs, pos1, pos2, pos3, out):
+    nc = tc.nc
+    with ExitStack() as ctx:
+        keep = ctx.enter_context(tc.tile_pool(name="keep", bufs=1))
+        ring = ctx.enter_context(tc.tile_pool(name="ring", bufs=3))
+        psum = ctx.enter_context(tc.psum_pool(name="psum", bufs=4))
+
+        offs_sb = keep.tile([P, S // STRIPE], U16, name="offs_sb")
+        nc.sync.dma_start(offs_sb[:], offs)
+
+        x_rows = xT.rearrange("(a p t) c -> a t p c", a=PASSES, t=PACK)
+        planes = {}
+        gate_sb = keep.tile([P, S], F32, name="gate_sb")
+
+        def load_plane(a, t):
+            planes[a, t] = keep.tile([P, T], F32, name="x_%d_%d" % (a, t))
+            nc.sync.dma_start(planes[a, t][:], x_rows[a, t])
+
+        def load_gate(i):
+            s0, n = GATE_LOADS[i]
+            nc.sync.dma_start(gate_sb[:, s0 : s0 + n], gate[0:P, s0 : s0 + n])
+
+        load_plane(0, 0)
+        load_gate(0)
+        load_gate(1)
+        for a in range(PASSES):
+            for t in range(PACK):
+                if (a, t) != (0, 0):
+                    load_plane(a, t)
+        load_gate(2)
+
+        w_scale_sb = keep.tile([P, E * PASSES * N], U8, name="w_scale_sb", align_bytes=64)
+        nc.gpsimd.memset(w_scale_sb[:].bitcast(I32), 0)
+        scale_rows = w_scales.bitcast(I32).rearrange("e a (q r) n -> r q (e a) n", r=4)
+        scale_dst = w_scale_sb[:].bitcast(I32).rearrange("p (g n) -> p g n", n=N // 4)
+        for r in range(4):
+            nc.sync.dma_start(scale_dst[r:P:32], scale_rows[r])
+
+        word_rows = w_words.bitcast(I32).rearrange("e a p n -> p (e a) n")
+        w_sb = []
+        for g in range(E // W_GROUP):
+            w_sb.append(keep.tile([P, W_GROUP * PASSES * 2 * N], U8, name="w_%d" % g, align_bytes=64))
+            nc.sync.dma_start(
+                w_sb[g][:].bitcast(I32).rearrange("p (g n) -> p g n", n=N // 2),
+                word_rows[:, g * W_GROUP * PASSES : (g + 1) * W_GROUP * PASSES, :],
+            )
+        b_sb = keep.tile([P, E], F32, name="b_sb")
+        nc.sync.dma_start(b_sb[:], b)
+        load_gate(3)
+        pos_sb = []
+        for r, pos in enumerate((pos1, pos2, pos3)):
+            pos_sb.append(keep.tile([P, T // STRIPE], U16, name="pos_%d" % r))
+            nc.sync.dma_start(pos_sb[r][:], pos)
+
+        y = keep.tile([P, S], F32, name="y")
+
+        def gather(u):
+            a, s0, n = UNITS[u]
+            gated = ring.tile([P, PACK, n], F32, name="gated")
+            for t in range(PACK):
+                cuts = GATE_LOADS[:2] if (u, t) == (0, 0) else [(s0, n)]
+                for c0, m in cuts:
+                    nc.vector.tensor_tensor(
+                        gated[:, t, c0 - s0 : c0 - s0 + m],
+                        planes[a, t][:].indirect(offs_sb[:, c0 // STRIPE : (c0 + m) // STRIPE]),
+                        gate_sb[:, c0 : c0 + m],
+                        MULT,
+                    )
+            grouped = ring.tile([P, n, PACK], BF16, name="grouped", align_bytes=64)
+            nc.scalar.copy(
+                grouped[:].rearrange("p (c i) t -> p c t i", i=4),
+                gated[:].rearrange("p t (c i) -> p c t i", i=4),
+            )
+            return grouped
+
+        codes = [keep.tile([P, S], U32, name="codes_%d" % a, align_bytes=64) for a in range(PASSES)]
+        scales = [keep.tile([P, S], U8, name="scales_%d" % a, align_bytes=64) for a in range(PASSES)]
+
+        def quantize(u, grouped):
+            a, s0, n = UNITS[u]
+            c0 = 0
+            for m in (1024, 512, 256, 128):
+                if n & m:
+                    cols = slice(s0 + c0, s0 + c0 + m)
+                    nc.vector.quantize_mx(
+                        codes[a][:, cols].bitcast(FP8X4),
+                        scales[a][:, cols],
+                        grouped[:, c0 : c0 + m, :].rearrange("p n t -> p (n t)"),
+                    )
+                    c0 = c0 + m
+
+        def multiply(u):
+            s0, n = UNITS[u][1:]
+            for e in range(s0 // C, (s0 + n + C - 1) // C):
+                lo, hi = max(s0, e * C), min(s0 + n, (e + 1) * C)
+                acc = psum.tile([P, hi - lo], F32, name="acc")
+                for c0 in range(lo, hi, P):
+                    for a in range(PASSES):
+                        g = (e % W_GROUP) * PASSES + a
+                        ge = e * PASSES + a
+                        nc.tensor.matmul_mx(
+                            acc[:, c0 - lo : c0 - lo + P],
+                            lhsT=w_sb[e // W_GROUP][:, g * 2 * N : (g + 1) * 2 * N].bitcast(FP4X4),
+                            lhsT_scale=w_scale_sb[:, ge * N : (ge + 1) * N],
+                            rhs=codes[a][:, c0 : c0 + P].bitcast(FP8X4),
+                            rhs_scale=scales[a][:, c0 : c0 + P],
+                            start=(a == 0),
+                            stop=(a == PASSES - 1),
+                        )
+                nc.scalar.activation(y[:, lo:hi], acc[:], IDENT, bias=b_sb[:, e : e + 1])
+
+        grouped_of = {}
+        for u in range(len(UNITS) + 1):
+            if u < len(UNITS):
+                grouped_of[u] = gather(u)
+            if u >= 1:
+                quantize(u - 1, grouped_of[u - 1])
+                if UNITS[u - 1][0] == PASSES - 1:
+                    multiply(u - 1)
+
+        def slots_of(r, t0, n):
+            return y[:].indirect(pos_sb[r][:, t0 // STRIPE : (t0 + n) // STRIPE])
+
+        first = keep.tile([P, T], F32, name="first")
+        second = keep.tile([P, T], F32, name="second")
+        for t0 in (0, HALF):
+            nc.vector.tensor_copy(first[:, t0 : t0 + HALF], slots_of(0, t0, HALF))
+        for t0 in (0, HALF):
+            nc.vector.tensor_tensor(second[:, t0 : t0 + HALF], slots_of(1, t0, HALF), first[:, t0 : t0 + HALF], ADD)
+        for j, (t0, n) in enumerate(OUT_PIECES):
+            total = keep.tile([P, n], F32, name="total_%d" % j)
+            nc.vector.tensor_tensor(total[:], slots_of(2, t0, n), second[:, t0 : t0 + n], ADD)
+            nc.sync.dma_start(out[:, t0 : t0 + n], total[:])

@@ -60,6 +60,7 @@ def tile_moe_pre_lin_bias_kernel(tc, xT, w_words, w_scales, b, gate, offs, pos1,
                 if (a, t) != (0, 0):
                     load_plane(a, t)
         load_gate(2)
+        load_gate(3)
 
         w_scale_sb = keep.tile([P, E * PASSES * N], U8, name="w_scale_sb", align_bytes=64)
         nc.gpsimd.memset(w_scale_sb[:].bitcast(I32), 0)
@@ -78,7 +79,6 @@ def tile_moe_pre_lin_bias_kernel(tc, xT, w_words, w_scales, b, gate, offs, pos1,
             )
         b_sb = keep.tile([P, E], F32, name="b_sb")
         nc.sync.dma_start(b_sb[:], b)
-        load_gate(3)
         pos_sb = []
         for r, pos in enumerate((pos1, pos2, pos3)):
             pos_sb.append(keep.tile([P, T // STRIPE], U16, name="pos_%d" % r))
@@ -88,7 +88,7 @@ def tile_moe_pre_lin_bias_kernel(tc, xT, w_words, w_scales, b, gate, offs, pos1,
 
         def gather(u):
             a, s0, n = UNITS[u]
-            gated = ring.tile([P, PACK, n], F32, name="gated")
+            gated = ring.tile([P, PACK, n], F32, name="gated", bufs=2)
             for t in range(PACK):
                 cuts = GATE_LOADS[:2] if (u, t) == (0, 0) else [(s0, n)]
                 for c0, m in cuts:

@@ -23,11 +23,17 @@ P = 128
 PACK = 4
 PASSES = K // (P * PACK)
 STRIPE = 16
-UNITS = [(0, 0, 1024), (1, 0, 1024), (0, 1024, 1024), (1, 1024, 1024), (0, 2048, 1024), (1, 2048, 1024), (0, 3072, 768), (1, 3072, 384), (1, 3456, 256), (1, 3712, 128)]
-GATE_LOADS = [(0, 256), (256, 768), (1024, 1024), (2048, 1792)]
+UNITS = [(0, 0, 2048), (1, 0, 1920), (0, 2048, 1792), (1, 1920, 1024), (1, 2944, 512), (1, 3456, 256), (1, 3712, 128)]
+GATE_LOADS = [(0, 256), (256, 640), (896, 1152), (2048, 1792)]
+WINDOWS = [2048 + STRIPE, 1920 + STRIPE]
 HALF = T // 2
 OUT_PIECES = [(0, 512), (512, 512), (1024, 256)]
 W_GROUP = 5
+
+
+def widths(n):
+    sizes = [1024] * (n // 1024) + [w for w in (512, 256, 128) if n % 1024 & w]
+    return [(sum(sizes[:j]), w) for j, w in enumerate(sizes)]
 
 
 def tile_moe_pre_lin_bias_kernel(tc, xT, w_words, w_scales, b, gate, offs, pos1, pos2, pos3, out):
@@ -45,21 +51,21 @@ def tile_moe_pre_lin_bias_kernel(tc, xT, w_words, w_scales, b, gate, offs, pos1,
         gate_sb = keep.tile([P, S], F32, name="gate_sb")
 
         def load_plane(a, t):
-            planes[a, t] = keep.tile([P, T], F32, name="x_%d_%d" % (a, t))
-            nc.sync.dma_start(planes[a, t][:], x_rows[a, t])
+            planes[a, t] = keep.tile([P, WINDOWS[a]], F32, name="x_%d_%d" % (a, t))
+            nc.gpsimd.memset(planes[a, t][:, T : WINDOWS[a]], 0.0)
+            nc.sync.dma_start(planes[a, t][:, 0:T], x_rows[a, t])
 
         def load_gate(i):
             s0, n = GATE_LOADS[i]
             nc.sync.dma_start(gate_sb[:, s0 : s0 + n], gate[0:P, s0 : s0 + n])
 
         load_plane(0, 0)
-        load_gate(0)
-        load_gate(1)
+        for i in range(3):
+            load_gate(i)
         for a in range(PASSES):
             for t in range(PACK):
                 if (a, t) != (0, 0):
                     load_plane(a, t)
-        load_gate(2)
         load_gate(3)
 
         w_scale_sb = keep.tile([P, E * PASSES * N], U8, name="w_scale_sb", align_bytes=64)
@@ -90,7 +96,7 @@ def tile_moe_pre_lin_bias_kernel(tc, xT, w_words, w_scales, b, gate, offs, pos1,
             a, s0, n = UNITS[u]
             gated = ring.tile([P, PACK, n], F32, name="gated", bufs=2)
             for t in range(PACK):
-                cuts = GATE_LOADS[:2] if (u, t) == (0, 0) else [(s0, n)]
+                cuts = GATE_LOADS[:3] if (u, t) == (0, 0) else [(s0, n)]
                 for c0, m in cuts:
                     nc.vector.tensor_tensor(
                         gated[:, t, c0 - s0 : c0 - s0 + m],
@@ -98,28 +104,27 @@ def tile_moe_pre_lin_bias_kernel(tc, xT, w_words, w_scales, b, gate, offs, pos1,
                         gate_sb[:, c0 : c0 + m],
                         MULT,
                     )
-            grouped = ring.tile([P, n, PACK], BF16, name="grouped", align_bytes=64)
-            nc.scalar.copy(
-                grouped[:].rearrange("p (c i) t -> p c t i", i=4),
-                gated[:].rearrange("p t (c i) -> p c t i", i=4),
-            )
-            return grouped
+            pieces = []
+            for c0, m in widths(n):
+                grouped = ring.tile([P, m, PACK], BF16, name="grouped", align_bytes=64, bufs=4)
+                nc.scalar.copy(
+                    grouped[:].rearrange("p (c i) t -> p c t i", i=4),
+                    gated[:, :, c0 : c0 + m].rearrange("p t (c i) -> p c t i", i=4),
+                )
+                pieces.append((s0 + c0, m, grouped))
+            return pieces
 
         codes = [keep.tile([P, S], U32, name="codes_%d" % a, align_bytes=64) for a in range(PASSES)]
         scales = [keep.tile([P, S], U8, name="scales_%d" % a, align_bytes=64) for a in range(PASSES)]
 
-        def quantize(u, grouped):
-            a, s0, n = UNITS[u]
-            c0 = 0
-            for m in (1024, 512, 256, 128):
-                if n & m:
-                    cols = slice(s0 + c0, s0 + c0 + m)
-                    nc.vector.quantize_mx(
-                        codes[a][:, cols].bitcast(FP8X4),
-                        scales[a][:, cols],
-                        grouped[:, c0 : c0 + m, :].rearrange("p n t -> p (n t)"),
-                    )
-                    c0 = c0 + m
+        def quantize(u, pieces):
+            a = UNITS[u][0]
+            for c0, m, grouped in pieces:
+                nc.vector.quantize_mx(
+                    codes[a][:, c0 : c0 + m].bitcast(FP8X4),
+                    scales[a][:, c0 : c0 + m],
+                    grouped[:].rearrange("p n t -> p (n t)"),
+                )
 
         def multiply(u):
             s0, n = UNITS[u][1:]
@@ -153,13 +158,13 @@ def tile_moe_pre_lin_bias_kernel(tc, xT, w_words, w_scales, b, gate, offs, pos1,
         def slots_of(r, t0, n):
             return y[:].indirect(pos_sb[r][:, t0 // STRIPE : (t0 + n) // STRIPE])
 
-        first = keep.tile([P, T], F32, name="first")
-        second = keep.tile([P, T], F32, name="second")
+        first = ring.tile([P, T], F32, name="grouped", align_bytes=64, bufs=4)
+        second = ring.tile([P, T], F32, name="grouped", align_bytes=64, bufs=4)
+        total = ring.tile([P, T], F32, name="grouped", align_bytes=64, bufs=4)
         for t0 in (0, HALF):
             nc.vector.tensor_copy(first[:, t0 : t0 + HALF], slots_of(0, t0, HALF))
         for t0 in (0, HALF):
             nc.vector.tensor_tensor(second[:, t0 : t0 + HALF], slots_of(1, t0, HALF), first[:, t0 : t0 + HALF], ADD)
-        for j, (t0, n) in enumerate(OUT_PIECES):
-            total = keep.tile([P, n], F32, name="total_%d" % j)
-            nc.vector.tensor_tensor(total[:], slots_of(2, t0, n), second[:, t0 : t0 + n], ADD)
-            nc.sync.dma_start(out[:, t0 : t0 + n], total[:])
+        for t0, n in OUT_PIECES:
+            nc.vector.tensor_tensor(total[:, t0 : t0 + n], slots_of(2, t0, n), second[:, t0 : t0 + n], ADD)
+            nc.sync.dma_start(out[:, t0 : t0 + n], total[:, t0 : t0 + n])

from contextlib import ExitStack

import concourse.mybir as mybir

K, T, E, C, N = 1024, 1280, 15, 256, 128
S = E * C
FLOPS = 2 * K * N * S
BYTES = 4 * K * T + E * K * N // 2 + E * K * N // 32 + 4 * N * E + 4 * S + 2 * 128 * (S + 3 * T) // 16 + 4 * N * T

F32 = mybir.dt.float32
BF16 = mybir.dt.bfloat16
I32 = mybir.dt.int32
U32 = mybir.dt.uint32
U16 = mybir.dt.uint16
U8 = mybir.dt.uint8
FP8X4 = mybir.dt.float8_e4m3fn_x4
FP4X4 = mybir.dt.float4_e2m1fn_x4
MULT = mybir.AluOpType.mult
ADD = mybir.AluOpType.add
IDENT = mybir.ActivationFunctionType.Identity

P = 128
PACK = 4
PASSES = K // (P * PACK)
STRIPE = 16
UNITS = [(0, 0, 2048), (1, 0, 1920), (0, 2048, 1792), (1, 1920, 1024), (1, 2944, 512), (1, 3456, 256), (1, 3712, 128)]
GATE_LOADS = [(0, 256), (256, 640), (896, 1152), (2048, 1792)]
WINDOWS = [2048 + STRIPE, 1920 + STRIPE]
HALF = T // 2
OUT_PIECES = [(0, 512), (512, 512), (1024, 256)]
W_GROUP = 5


def widths(n):
    sizes = [1024] * (n // 1024) + [w for w in (512, 256, 128) if n % 1024 & w]
    return [(sum(sizes[:j]), w) for j, w in enumerate(sizes)]


def tile_moe_pre_lin_bias_kernel(tc, xT, w_words, w_scales, b, gate, offs, pos1, pos2, pos3, out):
    nc = tc.nc
    with ExitStack() as ctx:
        keep = ctx.enter_context(tc.tile_pool(name="keep", bufs=1))
        ring = ctx.enter_context(tc.tile_pool(name="ring", bufs=3))
        psum = ctx.enter_context(tc.psum_pool(name="psum", bufs=4))

        offs_sb = keep.tile([P, S // STRIPE], U16, name="offs_sb")
        nc.sync.dma_start(offs_sb[:], offs)

        x_rows = xT.rearrange("(a p t) c -> a t p c", a=PASSES, t=PACK)
        planes = {}
        gate_sb = keep.tile([P, S], F32, name="gate_sb")

        def load_plane(a, t):
            planes[a, t] = keep.tile([P, WINDOWS[a]], F32, name="x_%d_%d" % (a, t))
            nc.gpsimd.memset(planes[a, t][:, T : WINDOWS[a]], 0.0)
            nc.sync.dma_start(planes[a, t][:, 0:T], x_rows[a, t])

        def load_gate(i):
            s0, n = GATE_LOADS[i]
            nc.sync.dma_start(gate_sb[:, s0 : s0 + n], gate[0:P, s0 : s0 + n])

        load_plane(0, 0)
        for i in range(3):
            load_gate(i)
        for a in range(PASSES):
            for t in range(PACK):
                if (a, t) != (0, 0):
                    load_plane(a, t)
        load_gate(3)

        w_scale_sb = keep.tile([P, E * PASSES * N], U8, name="w_scale_sb", align_bytes=64)
        nc.gpsimd.memset(w_scale_sb[:].bitcast(I32), 0)
        scale_rows = w_scales.bitcast(I32).rearrange("e a (q r) n -> r q (e a) n", r=4)
        scale_dst = w_scale_sb[:].bitcast(I32).rearrange("p (g n) -> p g n", n=N // 4)
        for r in range(4):
            nc.sync.dma_start(scale_dst[r:P:32], scale_rows[r])

        word_rows = w_words.bitcast(I32).rearrange("e a p n -> p (e a) n")
        w_sb = []
        for g in range(E // W_GROUP):
            w_sb.append(keep.tile([P, W_GROUP * PASSES * 2 * N], U8, name="w_%d" % g, align_bytes=64))
            nc.sync.dma_start(
                w_sb[g][:].bitcast(I32).rearrange("p (g n) -> p g n", n=N // 2),
                word_rows[:, g * W_GROUP * PASSES : (g + 1) * W_GROUP * PASSES, :],
            )
        b_sb = keep.tile([P, E], F32, name="b_sb")
        nc.sync.dma_start(b_sb[:], b)
        pos_sb = []
        for r, pos in enumerate((pos1, pos2, pos3)):
            pos_sb.append(keep.tile([P, T // STRIPE], U16, name="pos_%d" % r))
            nc.sync.dma_start(pos_sb[r][:], pos)

        y = keep.tile([P, S], F32, name="y")

        def gather(u):
            a, s0, n = UNITS[u]
            gated = ring.tile([P, PACK, n], F32, name="gated", bufs=2)
            for t in range(PACK):
                cuts = GATE_LOADS[:3] if (u, t) == (0, 0) else [(s0, n)]
                for c0, m in cuts:
                    nc.vector.tensor_tensor(
                        gated[:, t, c0 - s0 : c0 - s0 + m],
                        planes[a, t][:].indirect(offs_sb[:, c0 // STRIPE : (c0 + m) // STRIPE]),
                        gate_sb[:, c0 : c0 + m],
                        MULT,
                    )
            pieces = []
            for c0, m in widths(n):
                grouped = ring.tile([P, m, PACK], BF16, name="grouped", align_bytes=64, bufs=4)
                nc.scalar.copy(
                    grouped[:].rearrange("p (c i) t -> p c t i", i=4),
                    gated[:, :, c0 : c0 + m].rearrange("p t (c i) -> p c t i", i=4),
                )
                pieces.append((s0 + c0, m, grouped))
            return pieces

        codes = [keep.tile([P, S], U32, name="codes_%d" % a, align_bytes=64) for a in range(PASSES)]
        scales = [keep.tile([P, S], U8, name="scales_%d" % a, align_bytes=64) for a in range(PASSES)]

        def quantize(u, pieces):
            a = UNITS[u][0]
            for c0, m, grouped in pieces:
                nc.vector.quantize_mx(
                    codes[a][:, c0 : c0 + m].bitcast(FP8X4),
                    scales[a][:, c0 : c0 + m],
                    grouped[:].rearrange("p n t -> p (n t)"),
                )

        def multiply(u):
            s0, n = UNITS[u][1:]
            for e in range(s0 // C, (s0 + n + C - 1) // C):
                lo, hi = max(s0, e * C), min(s0 + n, (e + 1) * C)
                acc = psum.tile([P, hi - lo], F32, name="acc")
                for c0 in range(lo, hi, P):
                    for a in range(PASSES):
                        g = (e % W_GROUP) * PASSES + a
                        ge = e * PASSES + a
                        nc.tensor.matmul_mx(
                            acc[:, c0 - lo : c0 - lo + P],
                            lhsT=w_sb[e // W_GROUP][:, g * 2 * N : (g + 1) * 2 * N].bitcast(FP4X4),
                            lhsT_scale=w_scale_sb[:, ge * N : (ge + 1) * N],
                            rhs=codes[a][:, c0 : c0 + P].bitcast(FP8X4),
                            rhs_scale=scales[a][:, c0 : c0 + P],
                            start=(a == 0),
                            stop=(a == PASSES - 1),
                        )
                nc.scalar.activation(y[:, lo:hi], acc[:], IDENT, bias=b_sb[:, e : e + 1])

        grouped_of = {}
        for u in range(len(UNITS) + 1):
            if u < len(UNITS):
                grouped_of[u] = gather(u)
            if u >= 1:
                quantize(u - 1, grouped_of[u - 1])
                if UNITS[u - 1][0] == PASSES - 1:
                    multiply(u - 1)

        def slots_of(r, t0, n):
            return y[:].indirect(pos_sb[r][:, t0 // STRIPE : (t0 + n) // STRIPE])

        first = ring.tile([P, T], F32, name="grouped", align_bytes=64, bufs=4)
        second = ring.tile([P, T], F32, name="grouped", align_bytes=64, bufs=4)
        total = ring.tile([P, T], F32, name="grouped", align_bytes=64, bufs=4)
        for t0 in (0, HALF):
            nc.vector.tensor_copy(first[:, t0 : t0 + HALF], slots_of(0, t0, HALF))
        for t0 in (0, HALF):
            nc.vector.tensor_tensor(second[:, t0 : t0 + HALF], slots_of(1, t0, HALF), first[:, t0 : t0 + HALF], ADD)
        for t0, n in OUT_PIECES:
            nc.vector.tensor_tensor(total[:, t0 : t0 + n], slots_of(2, t0, n), second[:, t0 : t0 + n], ADD)
            nc.sync.dma_start(out[:, t0 : t0 + n], total[:, t0 : t0 + n])
